import numpy as np
import ml_dtypes

BF16 = ml_dtypes.bfloat16


def bf(x):
    return np.asarray(x, np.float32).astype(BF16)


def f32(x):
    return np.asarray(x, np.float32)


def f64(x):
    return np.asarray(x).astype(np.float64)


def striped(idx):
    return np.tile(idx.reshape(-1, 16).T, (8, 1))


S, A, K, M, N, E, Q = 512, 512, 256, 256, 128, 1, 128


def setup_inputs():
    return {"x": bf(np.random.standard_normal((A, S))), "wd": bf(np.random.standard_normal((A, M)) / np.sqrt(A)), "y": bf(np.random.standard_normal((K, N))), "w": bf(np.random.standard_normal((K, M)) / np.sqrt(K)), "b": f32(0.5 * np.random.standard_normal((M, 1))), "offs": striped(np.random.permutation(S)[:N])}


def reference(x, wd, y, w, b, offs):
    idx = offs[:16].T.reshape(-1)
    z = f64(wd).T @ f64(x)
    z[:, idx] += f64(w).T @ f64(y)
    return np.maximum(z + f64(b), 0.0)

@@ -1,0 +1,62 @@
+import concourse.mybir as mybir
+
+P = 128
+D, S, K, M, N = 512, 512, 256, 256, 128
+DENSE_BLOCKS = D // P
+EXPERT_BLOCKS = K // P
+WINDOWS = M // P
+
+BF16, F32, U16 = mybir.dt.bfloat16, mybir.dt.float32, mybir.dt.uint16
+RELU = mybir.ActivationFunctionType.Relu
+ADD, MAX = mybir.AluOpType.add, mybir.AluOpType.max
+
+FLOPS = 2 * D * M * S + 2 * K * M * N
+
+
+def tile_rows_fillproj_relu_kernel(tc, x, wd, y, w, b, offs, out):
+    nc = tc.nc
+    with (
+        tc.tile_pool(name="held", bufs=1) as held,
+        tc.psum_pool(name="psum", bufs=1) as psum,
+    ):
+        wd_tile = held.tile([P, DENSE_BLOCKS, M], BF16)
+        x_halves = [held.tile([P, DENSE_BLOCKS // 2, S], BF16, name=f"x_half{h}") for h in range(2)]
+        w_tile = held.tile([P, EXPERT_BLOCKS, M], BF16)
+        y_tile = held.tile([P, EXPERT_BLOCKS, N], BF16)
+        offsets = held.tile([P, N // 16], U16)
+        bias = held.tile([P, WINDOWS], F32)
+
+        x_rows = x.rearrange("(p a) s -> p a s", p=P)
+        nc.sync.dma_start(wd_tile[:], wd.rearrange("(p a) m -> p a m", p=P))
+        nc.sync.dma_start(x_halves[0][:], x_rows[:, 0 : DENSE_BLOCKS // 2, :])
+        nc.sync.dma_start(x_halves[1][:], x_rows[:, DENSE_BLOCKS // 2 : DENSE_BLOCKS, :])
+        nc.sync.dma_start(w_tile[:], w.rearrange("(p a) m -> p a m", p=P))
+        nc.sync.dma_start(y_tile[:], y.rearrange("(p a) n -> p a n", p=P))
+        nc.sync.dma_start(offsets[:], offs)
+        nc.scalar.dma_start(bias[:], b.rearrange("(v p) o -> p (v o)", p=P))
+
+        windows = [psum.tile([P, S], F32, name=f"window{v}") for v in range(WINDOWS)]
+
+        for a in range(DENSE_BLOCKS):
+            x_block = x_halves[a // 2][:, a % 2, :]
+            for v in range(WINDOWS):
+                nc.tensor.matmul(
+                    windows[v][:], wd_tile[:, a, v * P : (v + 1) * P], x_block, start=(a == 0), stop=False
+                )
+
+        for v in range(WINDOWS):
+            for a in range(EXPERT_BLOCKS):
+                nc.tensor.matmul(
+                    windows[v][:].indirect(offsets[:]),
+                    w_tile[:, a, v * P : (v + 1) * P],
+                    y_tile[:, a, :],
+                    start=False,
+                    stop=(a == EXPERT_BLOCKS - 1),
+                )
+
+        relu0 = held.tile([P, S], F32)
+        nc.vector.tensor_scalar(relu0[:], windows[0][:], bias[:, 0:1], 0.0, ADD, MAX)
+        nc.sync.dma_start(out[0:P, :], relu0[:])
+        relu1 = held.tile([P, S], F32)
+        nc.scalar.activation(relu1[:], windows[1][:], RELU, bias=bias[:, 1:2])
+        nc.scalar.dma_start(out[P : 2 * P, :], relu1[:])

@@ -10,6 +10,8 @@ BF16, F32, U16 = mybir.dt.bfloat16, mybir.dt.float32, mybir.dt.uint16
 RELU = mybir.ActivationFunctionType.Relu
 ADD, MAX = mybir.AluOpType.add, mybir.AluOpType.max
 
+WARM_UPS = 4
+
 FLOPS = 2 * D * M * S + 2 * K * M * N
 
 
@@ -20,7 +22,7 @@ def tile_rows_fillproj_relu_kernel(tc, x, wd, y, w, b, offs, out):
         tc.psum_pool(name="psum", bufs=1) as psum,
     ):
         wd_tile = held.tile([P, DENSE_BLOCKS, M], BF16)
-        x_halves = [held.tile([P, DENSE_BLOCKS // 2, S], BF16, name=f"x_half{h}") for h in range(2)]
+        x_blocks = [held.tile([P, S], BF16, name=f"x_block{a}") for a in range(DENSE_BLOCKS)]
         w_tile = held.tile([P, EXPERT_BLOCKS, M], BF16)
         y_tile = held.tile([P, EXPERT_BLOCKS, N], BF16)
         offsets = held.tile([P, N // 16], U16)
@@ -28,20 +30,27 @@ def tile_rows_fillproj_relu_kernel(tc, x, wd, y, w, b, offs, out):
 
         x_rows = x.rearrange("(p a) s -> p a s", p=P)
         nc.sync.dma_start(wd_tile[:], wd.rearrange("(p a) m -> p a m", p=P))
-        nc.sync.dma_start(x_halves[0][:], x_rows[:, 0 : DENSE_BLOCKS // 2, :])
-        nc.sync.dma_start(x_halves[1][:], x_rows[:, DENSE_BLOCKS // 2 : DENSE_BLOCKS, :])
+        for a in range(DENSE_BLOCKS):
+            nc.sync.dma_start(x_blocks[a][:], x_rows[:, a, :])
         nc.sync.dma_start(w_tile[:], w.rearrange("(p a) m -> p a m", p=P))
         nc.sync.dma_start(y_tile[:], y.rearrange("(p a) n -> p a n", p=P))
         nc.sync.dma_start(offsets[:], offs)
-        nc.scalar.dma_start(bias[:], b.rearrange("(v p) o -> p (v o)", p=P))
+        nc.sync.dma_start(bias[:], b.rearrange("(v p) o -> p (v o)", p=P))
+
+        zeros = held.tile([P, S], BF16)
+        nc.vector.memset(zeros[:], 0.0)
+        early = held.tile([P, 1], F32)
+        nc.scalar.activation(early[:], zeros[:, 0:1], RELU)
+        spare_bank = psum.tile([P, S], F32)
+        for i in range(WARM_UPS):
+            nc.tensor.matmul(spare_bank[:], zeros[:, 0:P], zeros[:], start=True, stop=True)
 
         windows = [psum.tile([P, S], F32, name=f"window{v}") for v in range(WINDOWS)]
 
         for a in range(DENSE_BLOCKS):
-            x_block = x_halves[a // 2][:, a % 2, :]
             for v in range(WINDOWS):
                 nc.tensor.matmul(
-                    windows[v][:], wd_tile[:, a, v * P : (v + 1) * P], x_block, start=(a == 0), stop=False
+                    windows[v][:], wd_tile[:, a, v * P : (v + 1) * P], x_blocks[a][:], start=(a == 0), stop=False
                 )
 
         for v in range(WINDOWS):
@@ -54,9 +63,12 @@ def tile_rows_fillproj_relu_kernel(tc, x, wd, y, w, b, offs, out):
                     stop=(a == EXPERT_BLOCKS - 1),
                 )
 
-        relu0 = held.tile([P, S], F32)
-        nc.vector.tensor_scalar(relu0[:], windows[0][:], bias[:, 0:1], 0.0, ADD, MAX)
-        nc.sync.dma_start(out[0:P, :], relu0[:])
-        relu1 = held.tile([P, S], F32)
-        nc.scalar.activation(relu1[:], windows[1][:], RELU, bias=bias[:, 1:2])
-        nc.scalar.dma_start(out[P : 2 * P, :], relu1[:])
+        HALF = S // 2
+        relu0 = [held.tile([P, HALF], F32, name=f"relu0_{h}") for h in range(2)]
+        relu1 = [held.tile([P, HALF], F32, name=f"relu1_{h}") for h in range(2)]
+        for h in range(2):
+            columns = slice(h * HALF, (h + 1) * HALF)
+            nc.vector.tensor_scalar(relu0[h][:], windows[0][:, columns], bias[:, 0:1], 0.0, ADD, MAX)
+            nc.sync.dma_start(out[0:P, columns], relu0[h][:])
+            nc.scalar.activation(relu1[h][:], windows[1][:, columns], RELU, bias=bias[:, 1:2])
+            nc.scalar.dma_start(out[P : 2 * P, columns], relu1[h][:])

@@ -10,7 +10,7 @@ BF16, F32, U16 = mybir.dt.bfloat16, mybir.dt.float32, mybir.dt.uint16
 RELU = mybir.ActivationFunctionType.Relu
 ADD, MAX = mybir.AluOpType.add, mybir.AluOpType.max
 
-WARM_UPS = 4
+WARM_UPS, WARM_COLUMNS = 7, 256
 
 FLOPS = 2 * D * M * S + 2 * K * M * N
 
@@ -21,7 +21,7 @@ def tile_rows_fillproj_relu_kernel(tc, x, wd, y, w, b, offs, out):
         tc.tile_pool(name="held", bufs=1) as held,
         tc.psum_pool(name="psum", bufs=1) as psum,
     ):
-        wd_tile = held.tile([P, DENSE_BLOCKS, M], BF16)
+        wd_halves = [held.tile([P, DENSE_BLOCKS // 2, M], BF16, name=f"wd_half{h}") for h in range(2)]
         x_blocks = [held.tile([P, S], BF16, name=f"x_block{a}") for a in range(DENSE_BLOCKS)]
         w_tile = held.tile([P, EXPERT_BLOCKS, M], BF16)
         y_tile = held.tile([P, EXPERT_BLOCKS, N], BF16)
@@ -29,19 +29,21 @@ def tile_rows_fillproj_relu_kernel(tc, x, wd, y, w, b, offs, out):
         bias = held.tile([P, WINDOWS], F32)
 
         x_rows = x.rearrange("(p a) s -> p a s", p=P)
-        nc.sync.dma_start(wd_tile[:], wd.rearrange("(p a) m -> p a m", p=P))
+        wd_rows = wd.rearrange("(p a) m -> p a m", p=P)
         for a in range(DENSE_BLOCKS):
+            if a % 2 == 0:
+                nc.sync.dma_start(wd_halves[a // 2][:], wd_rows[:, a : a + 2, :])
             nc.sync.dma_start(x_blocks[a][:], x_rows[:, a, :])
         nc.sync.dma_start(w_tile[:], w.rearrange("(p a) m -> p a m", p=P))
         nc.sync.dma_start(y_tile[:], y.rearrange("(p a) n -> p a n", p=P))
         nc.sync.dma_start(offsets[:], offs)
         nc.sync.dma_start(bias[:], b.rearrange("(v p) o -> p (v o)", p=P))
 
-        zeros = held.tile([P, S], BF16)
+        zeros = held.tile([P, WARM_COLUMNS], BF16)
         nc.vector.memset(zeros[:], 0.0)
         early = held.tile([P, 1], F32)
         nc.scalar.activation(early[:], zeros[:, 0:1], RELU)
-        spare_bank = psum.tile([P, S], F32)
+        spare_bank = psum.tile([P, WARM_COLUMNS], F32)
         for i in range(WARM_UPS):
             nc.tensor.matmul(spare_bank[:], zeros[:, 0:P], zeros[:], start=True, stop=True)
 
@@ -50,7 +52,7 @@ def tile_rows_fillproj_relu_kernel(tc, x, wd, y, w, b, offs, out):
         for a in range(DENSE_BLOCKS):
             for v in range(WINDOWS):
                 nc.tensor.matmul(
-                    windows[v][:], wd_tile[:, a, v * P : (v + 1) * P], x_blocks[a][:], start=(a == 0), stop=False
+                    windows[v][:], wd_halves[a // 2][:, a % 2, v * P : (v + 1) * P], x_blocks[a][:], start=(a == 0), stop=False
                 )
 
         for v in range(WINDOWS):

import concourse.mybir as mybir

P = 128
D, S, K, M, N = 512, 512, 256, 256, 128
DENSE_BLOCKS = D // P
EXPERT_BLOCKS = K // P
WINDOWS = M // P

BF16, F32, U16 = mybir.dt.bfloat16, mybir.dt.float32, mybir.dt.uint16
RELU = mybir.ActivationFunctionType.Relu
ADD, MAX = mybir.AluOpType.add, mybir.AluOpType.max

WARM_UPS, WARM_COLUMNS = 7, 256

FLOPS = 2 * D * M * S + 2 * K * M * N


def tile_rows_fillproj_relu_kernel(tc, x, wd, y, w, b, offs, out):
    nc = tc.nc
    with (
        tc.tile_pool(name="held", bufs=1) as held,
        tc.psum_pool(name="psum", bufs=1) as psum,
    ):
        wd_halves = [held.tile([P, DENSE_BLOCKS // 2, M], BF16, name=f"wd_half{h}") for h in range(2)]
        x_blocks = [held.tile([P, S], BF16, name=f"x_block{a}") for a in range(DENSE_BLOCKS)]
        w_tile = held.tile([P, EXPERT_BLOCKS, M], BF16)
        y_tile = held.tile([P, EXPERT_BLOCKS, N], BF16)
        offsets = held.tile([P, N // 16], U16)
        bias = held.tile([P, WINDOWS], F32)

        x_rows = x.rearrange("(p a) s -> p a s", p=P)
        wd_rows = wd.rearrange("(p a) m -> p a m", p=P)
        for a in range(DENSE_BLOCKS):
            if a % 2 == 0:
                nc.sync.dma_start(wd_halves[a // 2][:], wd_rows[:, a : a + 2, :])
            nc.sync.dma_start(x_blocks[a][:], x_rows[:, a, :])
        nc.sync.dma_start(w_tile[:], w.rearrange("(p a) m -> p a m", p=P))
        nc.sync.dma_start(y_tile[:], y.rearrange("(p a) n -> p a n", p=P))
        nc.sync.dma_start(offsets[:], offs)
        nc.sync.dma_start(bias[:], b.rearrange("(v p) o -> p (v o)", p=P))

        zeros = held.tile([P, WARM_COLUMNS], BF16)
        nc.vector.memset(zeros[:], 0.0)
        early = held.tile([P, 1], F32)
        nc.scalar.activation(early[:], zeros[:, 0:1], RELU)
        spare_bank = psum.tile([P, WARM_COLUMNS], F32)
        for i in range(WARM_UPS):
            nc.tensor.matmul(spare_bank[:], zeros[:, 0:P], zeros[:], start=True, stop=True)

        windows = [psum.tile([P, S], F32, name=f"window{v}") for v in range(WINDOWS)]

        for a in range(DENSE_BLOCKS):
            for v in range(WINDOWS):
                nc.tensor.matmul(
                    windows[v][:], wd_halves[a // 2][:, a % 2, v * P : (v + 1) * P], x_blocks[a][:], start=(a == 0), stop=False
                )

        for v in range(WINDOWS):
            for a in range(EXPERT_BLOCKS):
                nc.tensor.matmul(
                    windows[v][:].indirect(offsets[:]),
                    w_tile[:, a, v * P : (v + 1) * P],
                    y_tile[:, a, :],
                    start=False,
                    stop=(a == EXPERT_BLOCKS - 1),
                )

        HALF = S // 2
        relu0 = [held.tile([P, HALF], F32, name=f"relu0_{h}") for h in range(2)]
        relu1 = [held.tile([P, HALF], F32, name=f"relu1_{h}") for h in range(2)]
        for h in range(2):
            columns = slice(h * HALF, (h + 1) * HALF)
            nc.vector.tensor_scalar(relu0[h][:], windows[0][:, columns], bias[:, 0:1], 0.0, ADD, MAX)
            nc.sync.dma_start(out[0:P, columns], relu0[h][:])
            nc.scalar.activation(relu1[h][:], windows[1][:, columns], RELU, bias=bias[:, 1:2])
            nc.scalar.dma_start(out[P : 2 * P, columns], relu1[h][:])
